import numpy as np, ml_dtypes
CORES = [34,162,290,418,42,426]
N = 6
VB, TK = 1, 64
def setup_inputs(rng):
    h = rng.standard_normal((128, TK), dtype=np.float32) / 4; w = rng.standard_normal((N, 128, VB * 128), dtype=np.float32)
    a = 2 * np.pi * rng.random((TK)); s = 400 * rng.random((TK)) ** 1.5; h[0] = s * np.cos(a); h[1] = s * np.sin(a); h[2] = 150 * rng.standard_normal((TK)); w[:, 2, :] = 1 + w[:, 2, :] / 50
    a = (2 * np.pi * rng.random() + np.pi / 2 * (rng.permutation(N).reshape(N, 1, 1) + 0.5) / N - 0.5 + (np.arange(VB).reshape(1, VB, 1) + rng.random((N, VB, 128))) / VB).reshape(N, VB * 128); w[:, 0, :] = np.cos(a); w[:, 1, :] = np.sin(a)
    tgt = rng.integers(0, N * VB * 128, size=TK)
    oh = np.zeros((N * VB * 128, TK), np.float32); oh[tgt, np.arange(TK)] = 1.0
    oh = oh.reshape(N, VB, 128, TK).transpose(0, 2, 1, 3).reshape(N, 128, VB * TK)
    return {"h": np.broadcast_to(h, (N, 128, TK)).astype(ml_dtypes.bfloat16), "w": w.astype(ml_dtypes.bfloat16), "oh": oh.astype(ml_dtypes.bfloat16)}
def reference(h, w, oh):
    H, W, OH = h.astype(np.float64), w.astype(np.float64), oh.astype(np.float64)
    Z = np.concatenate([W[r].T @ H[r] for r in range(N)], axis=0)
    O = np.concatenate([OH[r][:, TK * b:TK * b + TK] for r in range(N) for b in range(VB)], axis=0)
    m = Z.max(axis=0)
    P = np.exp(Z - m); P = P / P.sum(axis=0)
    G = P - O
    d = sum(W[r] @ G[VB * 128 * r:VB * 128 * (r + 1)] for r in range(N)).astype(ml_dtypes.bfloat16)
    return {"d": np.broadcast_to(d, (N,) + d.shape)}

@@ -1,0 +1,184 @@
+from concourse.bass import DstId, RemoteDMATransfer
+from concourse.mybir import AluOpType, AxisListType, ActivationFunctionType
+
+SLOT = 136
+NS = 48
+
+SCRATCH = {
+    "own":   ("sbuf", [128, 256], "bfloat16"),
+    "land":  ("sbuf", [128, 256], "bfloat16"),
+    "hb":    ("sbuf", [128, 64], "bfloat16"),
+    "ones":  ("sbuf", [128, 128], "bfloat16"),
+    "ident": ("sbuf", [128, 128], "bfloat16"),
+    "sel":   ("sbuf", [128, 64], "bfloat16"),
+    "wto":   ("sbuf", [128, 136], "bfloat16"),
+    "wtp":   ("sbuf", [128, 136], "bfloat16"),
+    "eto":   ("sbuf", [128, 128], "bfloat16"),
+    "etp":   ("sbuf", [128, 128], "bfloat16"),
+    "nmo":   ("sbuf", [128, 8], "bfloat16"),
+    "acol":  ("sbuf", [128, 4], "float32"),
+    "tmp":   ("sbuf", [128, 132], "float32"),
+    "X":     ("sbuf", [128, 3 * SLOT], "bfloat16"),
+    "nmf":   ("sbuf", [128, 4], "float32"),
+    "ex":    ("sbuf", [128, 4], "float32"),
+    "es":    ("sbuf", [128, 4], "float32"),
+    "ssum":  ("sbuf", [128, 4], "float32"),
+    "rs":    ("sbuf", [128, 4], "float32"),
+    "D":     ("sbuf", [128, 192], "bfloat16"),
+    "dsb":   ("sbuf", [128, 64], "bfloat16"),
+    "zto":   ("psum", [128, 512], "float32"),
+    "ztp":   ("psum", [128, 512], "float32"),
+    "uo":    ("psum", [128, 512], "float32"),
+    "up":    ("psum", [128, 512], "float32"),
+    "wtops": ("psum", [128, 1024], "bfloat16"),
+    "wtpps": ("psum", [128, 1024], "bfloat16"),
+    "eops":  ("psum", [128, 1024], "bfloat16"),
+    "epps":  ("psum", [128, 1024], "bfloat16"),
+}
+SEMAPHORES = ["ld_w", "ld_oh", "ld_h", "arr1", "arr2", "sent", "stored"] + ["s%d" % i for i in range(NS)]
+
+
+def _bits(mask):
+    return [b for b in range(16) if (mask >> b) & 1]
+
+
+def rank_program(g, core, T, topo):
+    if T.rank_of(core) is None:
+        return
+    V, S, PE, SY = g.vector, g.scalar, g.tensor, g.sync
+    A, EXP, AX = AluOpType, ActivationFunctionType.Exp, AxisListType.X
+    sem = T.sem
+    cnt = [0]
+
+    def new():
+        cnt[0] += 1
+        return sem["s%d" % (cnt[0] - 1)]
+
+    def wait(q, *sems):
+        for s in sems:
+            q.wait_ge(s, 1)
+
+    my_rack = topo.rack(topo.host(core))
+    group = [c for c in T.cores if topo.rack(topo.host(c)) == my_rack]
+    partner = [c for c in T.cores if topo.rack(topo.host(c)) != my_rack
+               and topo.chip(c) == topo.chip(core) and topo.may_write(core, c)][0]
+    peers = [c for c in group if c != core]
+    o = group.index(core) * SLOT
+
+    own, land, hb, ident, X = T.own, T.land, T.hb, T.ident, T.X
+    nM = X[:, o + 129:o + 130]
+    nM_t = X[0:64, o + 129:o + 130]
+
+    SY.dma_start(own[:, 128:256], T.w[:]).then_inc(sem.ld_w, 16)
+    S.dma_start(own[:, 64:128], T.oh[:]).then_inc(sem.ld_oh, 16)
+    SY.dma_start(hb[:], T.h[:]).then_inc(sem.ld_h, 16)
+
+    s_ones, s_id, s_c1, s_c2, s_c3, s_c4, s_sel = new(), new(), new(), new(), new(), new(), new()
+    V.memset(T.ones[:], 1.0).then_inc(s_ones, 1)
+    wait(g, s_ones)
+    g.affine_select(ident[:], T.ones[:], [[-1, 128]], A.is_equal, 0.0, 0, 1).then_inc(s_id, 1)
+    V.memset(T.wto[:, 128:129], 1.0).then_inc(s_c1, 1)
+    V.memset(T.wtp[:, 128:129], 1.0).then_inc(s_c2, 1)
+    V.memset(T.nmo[64:128, 0:1], 0.0).then_inc(s_c3, 1)
+    V.memset(X[64:128, o + 129:o + 130], 0.0).then_inc(s_c4, 1)
+    wait(V, s_id)
+    V.tensor_tensor(T.sel[:], ident[:, 0:64], ident[:, 64:128], A.subtract).then_inc(s_sel, 1)
+
+    g.wait_ge(sem.ld_w, 16)
+    g.wait_ge(sem.ld_oh, 16)
+    rid, pid = topo.addr(partner, core)
+    m1 = topo.mask(core, partner)
+    n1 = len(_bits(m1))
+    g.remote_dma(out_ap=land[:, 64:256], in_ap=own[:, 64:256], remote_sem=sem.arr1, local_sem=sem.sent,
+                 pid=pid, routing_id=rid, dma_engine_mask=m1)
+
+    s_zto, s_wtops, s_nmo, s_eto, s_wto, s_mcol, s_eops, s_eo, s_uo = (new() for _ in range(9))
+    PE.wait_ge(sem.ld_w, 16)
+    PE.wait_ge(sem.ld_h, 16)
+    PE.matmul(T.zto[0:64, 0:128], hb[:], own[:, 128:256], True, True).then_inc(s_zto, 1)
+    wait(PE, s_id)
+    PE.transpose(T.wtops[:, 0:128], own[:, 128:256], ident[:]).then_inc(s_wtops, 1)
+    wait(V, s_zto)
+    V.tensor_reduce(T.nmo[0:64, 0:1], T.zto[0:64, 0:128], AX, A.max, negate=True).then_inc(s_nmo, 1)
+    wait(S, s_zto, s_nmo)
+    S.activation(T.eto[0:64, :], T.zto[0:64, 0:128], EXP, bias=T.nmo[0:64, 0:1], scale=1.0).then_inc(s_eto, 1)
+    wait(V, s_wtops)
+    V.tensor_copy(T.wto[:, 0:128], T.wtops[:, 0:128]).then_inc(s_wto, 1)
+    wait(V, s_nmo)
+    V.tensor_scalar(T.ztp[0:64, 128:129], T.nmo[0:64, 0:1], -1.0, None, A.mult).then_inc(s_mcol, 1)
+    wait(PE, s_eto)
+    PE.transpose(T.eops[:, 0:64], T.eto[0:64, :], ident[0:64, 0:64]).then_inc(s_eops, 1)
+    wait(V, s_eops)
+    V.tensor_copy(own[:, 0:64], T.eops[:, 0:64]).then_inc(s_eo, 1)
+    wait(PE, s_eo, s_wto, s_c1)
+    PE.wait_ge(sem.ld_oh, 16)
+    PE.matmul(T.uo[:, 0:129], own[:, 0:128], T.wto[:, 0:129], True, True).then_inc(s_uo, 1)
+
+    s_ztp, s_wtpps, s_nM, s_etp, s_a, s_wtp, s_epps, s_ep, s_up, s_tmp, s_msg = (new() for _ in range(11))
+    PE.wait_ge(sem.arr1, n1)
+    wait(PE, s_mcol)
+    PE.matmul(T.ztp[0:64, 0:128], hb[:], land[:, 128:256], True, True).then_inc(s_ztp, 1)
+    PE.transpose(T.wtpps[:, 0:128], land[:, 128:256], ident[:]).then_inc(s_wtpps, 1)
+    wait(V, s_ztp, s_mcol)
+    V.tensor_reduce(nM_t, T.ztp[0:64, 0:129], AX, A.max, negate=True).then_inc(s_nM, 1)
+    wait(S, s_ztp, s_nM)
+    S.activation(T.etp[0:64, :], T.ztp[0:64, 0:128], EXP, bias=nM_t, scale=1.0).then_inc(s_etp, 1)
+    wait(S, s_c3, s_c4)
+    S.activation(T.acol[:, 0:1], T.nmo[:, 0:1], EXP, bias=nM, scale=-1.0).then_inc(s_a, 1)
+    wait(V, s_wtpps)
+    V.tensor_copy(T.wtp[:, 0:128], T.wtpps[:, 0:128]).then_inc(s_wtp, 1)
+    wait(PE, s_etp)
+    PE.transpose(T.epps[:, 0:64], T.etp[0:64, :], ident[0:64, 0:64]).then_inc(s_epps, 1)
+    wait(V, s_epps)
+    V.tensor_copy(land[:, 0:64], T.epps[:, 0:64]).then_inc(s_ep, 1)
+    wait(PE, s_ep, s_wtp, s_c2)
+    PE.matmul(T.up[:, 0:129], land[:, 0:128], T.wtp[:, 0:129], True, True).then_inc(s_up, 1)
+    wait(V, s_a, s_uo)
+    V.tensor_scalar(T.tmp[:, 0:129], T.uo[:, 0:129], T.acol[:, 0:1], None, A.mult).then_inc(s_tmp, 1)
+    wait(V, s_up, s_tmp)
+    V.tensor_tensor(X[:, o:o + 129], T.up[:, 0:129], T.tmp[:, 0:129], A.add).then_inc(s_msg, 1)
+
+    wait(g, s_msg, s_nM, s_c4)
+    bits = _bits(topo.mask(core, peers[0]) & topo.mask(core, peers[1]))
+    half = len(bits) // 2
+    transfers = []
+    for j, p in enumerate(peers):
+        rid, pid = topo.addr(p, core)
+        transfers.append(RemoteDMATransfer(dst_ids=[DstId(rid=rid, pnc=pid)],
+                                           dma_engine_mask=sum(1 << b for b in bits[j * half:(j + 1) * half]),
+                                           remote_sem=sem.arr2, src=X[:, o:o + 130], dst=X[:, o:o + 130]))
+    g.remote_dma_fused(transfers, local_sem=sem.sent)
+
+    s_f1, s_ex, s_es, s_ss, s_rs, s_dsb = (new() for _ in range(6))
+    s_D = [new() for _ in range(3)]
+    s_mm = [new() for _ in range(3)]
+    nms = X[:, 129:3 * SLOT:SLOT]
+    sms = X[:, 128:3 * SLOT:SLOT]
+    V.wait_ge(sem.arr2, 2 * half)
+    wait(V, s_msg, s_nM, s_c4)
+    V.tensor_reduce(T.nmf[:, 0:1], nms, AX, A.min).then_inc(s_f1, 1)
+    S.wait_ge(sem.arr2, 2 * half)
+    wait(S, s_f1)
+    S.activation(T.ex[:, 0:3], nms, EXP, bias=T.nmf[:, 0:1], scale=-1.0).then_inc(s_ex, 1)
+    wait(V, s_ex)
+    V.tensor_tensor(T.es[:, 0:3], T.ex[:, 0:3], sms, A.mult).then_inc(s_es, 1)
+    wait(V, s_es)
+    V.tensor_reduce(T.ssum[:, 0:1], T.es[:, 0:3], AX, A.add).then_inc(s_ss, 1)
+    wait(V, s_ss)
+    V.reciprocal(T.rs[:, 0:1], T.ssum[:, 0:1]).then_inc(s_rs, 1)
+    wait(V, s_rs, s_sel)
+    for k in range(3):
+        V.tensor_scalar(T.D[:, 64 * k:64 * k + 64], T.sel[:], T.ex[:, k:k + 1], T.rs[:, 0:1],
+                        A.mult, A.mult).then_inc(s_D[k], 1)
+    PE.wait_ge(sem.arr2, 2 * half)
+    wait(PE, s_msg, s_nmo)
+    for k in range(3):
+        wait(PE, s_D[k])
+        PE.matmul(T.zto[:, 0:64], X[:, k * SLOT:k * SLOT + 128], T.D[:, 64 * k:64 * k + 64],
+                  k == 0, k == 2).then_inc(s_mm[k], 1)
+    wait(V, *s_mm)
+    V.tensor_copy(T.dsb[:], T.zto[:, 0:64]).then_inc(s_dsb, 1)
+    wait(SY, s_dsb)
+    SY.dma_start(T.d[:], T.dsb[:]).then_inc(sem.stored, 16)
+    SY.wait_ge(sem.stored, 16)
+    g.wait_ge(sem.sent, n1 + 2 * half)

@@ -2,14 +2,17 @@ from concourse.bass import DstId, RemoteDMATransfer
 from concourse.mybir import AluOpType, AxisListType, ActivationFunctionType
 
 SLOT = 136
-NS = 48
+NS = 56
 
 SCRATCH = {
-    "own":   ("sbuf", [128, 256], "bfloat16"),
-    "land":  ("sbuf", [128, 256], "bfloat16"),
+    "own":   ("sbuf", [128, 264], "bfloat16"),
+    "land":  ("sbuf", [128, 264], "bfloat16"),
     "hb":    ("sbuf", [128, 64], "bfloat16"),
     "ones":  ("sbuf", [128, 128], "bfloat16"),
+    "zc":    ("sbuf", [128, 8], "bfloat16"),
     "ident": ("sbuf", [128, 128], "bfloat16"),
+    "iocol": ("sbuf", [128, 8], "bfloat16"),
+    "iorow": ("sbuf", [128, 128], "bfloat16"),
     "sel":   ("sbuf", [128, 64], "bfloat16"),
     "wto":   ("sbuf", [128, 136], "bfloat16"),
     "wtp":   ("sbuf", [128, 136], "bfloat16"),
@@ -35,7 +38,7 @@ SCRATCH = {
     "eops":  ("psum", [128, 1024], "bfloat16"),
     "epps":  ("psum", [128, 1024], "bfloat16"),
 }
-SEMAPHORES = ["ld_w", "ld_oh", "ld_h", "arr1", "arr2", "sent", "stored"] + ["s%d" % i for i in range(NS)]
+SEMAPHORES = ["ld_w", "ld_oh", "ld_h", "arr1", "arr1b", "arr2", "sent", "stored"] + ["s%d" % i for i in range(NS)]
 
 
 def _bits(mask):
@@ -73,23 +76,37 @@ def rank_program(g, core, T, topo):
     S.dma_start(own[:, 64:128], T.oh[:]).then_inc(sem.ld_oh, 16)
     SY.dma_start(hb[:], T.h[:]).then_inc(sem.ld_h, 16)
 
-    s_ones, s_id, s_c1, s_c2, s_c3, s_c4, s_sel = new(), new(), new(), new(), new(), new(), new()
+    s_ones, s_id, s_c1, s_c2, s_c3, s_c4, s_sel, s_z0, s_ioc, s_ior, s_zc = (new() for _ in range(11))
+    g.iota(T.iocol[:, 0:1], [[0, 1]], 1, 1, allow_small_or_imprecise_dtypes=True).then_inc(s_ioc, 1)
     V.memset(T.ones[:], 1.0).then_inc(s_ones, 1)
+    V.memset(T.zc[:, 0:1], 0.0).then_inc(s_zc, 1)
+    V.memset(own[:, 0:64], 0.0).then_inc(s_z0, 1)
     wait(g, s_ones)
     g.affine_select(ident[:], T.ones[:], [[-1, 128]], A.is_equal, 0.0, 0, 1).then_inc(s_id, 1)
-    V.memset(T.wto[:, 128:129], 1.0).then_inc(s_c1, 1)
-    V.memset(T.wtp[:, 128:129], 1.0).then_inc(s_c2, 1)
+    wait(S, s_zc)
+    S.activation(T.wto[:, 128:129], T.zc[:, 0:1], EXP).then_inc(s_c1, 1)
+    S.activation(T.wtp[:, 128:129], T.zc[:, 0:1], EXP).then_inc(s_c2, 1)
     V.memset(T.nmo[64:128, 0:1], 0.0).then_inc(s_c3, 1)
     V.memset(X[64:128, o + 129:o + 130], 0.0).then_inc(s_c4, 1)
-    wait(V, s_id)
-    V.tensor_tensor(T.sel[:], ident[:, 0:64], ident[:, 64:128], A.subtract).then_inc(s_sel, 1)
 
-    g.wait_ge(sem.ld_w, 16)
-    g.wait_ge(sem.ld_oh, 16)
     rid, pid = topo.addr(partner, core)
     m1 = topo.mask(core, partner)
     n1 = len(_bits(m1))
-    g.remote_dma(out_ap=land[:, 64:256], in_ap=own[:, 64:256], remote_sem=sem.arr1, local_sem=sem.sent,
+    g.wait_ge(sem.ld_w, 16)
+    g.remote_dma(out_ap=land[:, 128:256], in_ap=own[:, 128:256], remote_sem=sem.arr1, local_sem=sem.sent,
+                 pid=pid, routing_id=rid, dma_engine_mask=m1)
+    g.iota(T.iorow[:], [[1, 128]], 1, 0, allow_small_or_imprecise_dtypes=True).then_inc(s_ior, 1)
+
+    s_ips, s_idx = new(), new()
+    PE.wait_ge(sem.ld_oh, 16)
+    wait(PE, s_z0, s_ioc)
+    PE.matmul(T.up[:, 256:257], own[:, 0:128], T.iocol[:, 0:1], True, True).then_inc(s_ips, 1)
+    wait(V, s_ips)
+    V.tensor_copy(own[:, 256:257], T.up[:, 256:257]).then_inc(s_idx, 1)
+    wait(V, s_id)
+    V.tensor_tensor(T.sel[:], ident[:, 0:64], ident[:, 64:128], A.subtract).then_inc(s_sel, 1)
+    wait(g, s_idx)
+    g.remote_dma(out_ap=land[:, 256:257], in_ap=own[:, 256:257], remote_sem=sem.arr1b, local_sem=sem.sent,
                  pid=pid, routing_id=rid, dma_engine_mask=m1)
 
     s_zto, s_wtops, s_nmo, s_eto, s_wto, s_mcol, s_eops, s_eo, s_uo = (new() for _ in range(9))
@@ -108,13 +125,12 @@ def rank_program(g, core, T, topo):
     V.tensor_scalar(T.ztp[0:64, 128:129], T.nmo[0:64, 0:1], -1.0, None, A.mult).then_inc(s_mcol, 1)
     wait(PE, s_eto)
     PE.transpose(T.eops[:, 0:64], T.eto[0:64, :], ident[0:64, 0:64]).then_inc(s_eops, 1)
-    wait(V, s_eops)
+    wait(V, s_eops, s_z0)
     V.tensor_copy(own[:, 0:64], T.eops[:, 0:64]).then_inc(s_eo, 1)
     wait(PE, s_eo, s_wto, s_c1)
-    PE.wait_ge(sem.ld_oh, 16)
     PE.matmul(T.uo[:, 0:129], own[:, 0:128], T.wto[:, 0:129], True, True).then_inc(s_uo, 1)
 
-    s_ztp, s_wtpps, s_nM, s_etp, s_a, s_wtp, s_epps, s_ep, s_up, s_tmp, s_msg = (new() for _ in range(11))
+    s_ztp, s_wtpps, s_nM, s_etp, s_ohp, s_a, s_wtp, s_epps, s_ep, s_up, s_tmp, s_msg = (new() for _ in range(12))
     PE.wait_ge(sem.arr1, n1)
     wait(PE, s_mcol)
     PE.matmul(T.ztp[0:64, 0:128], hb[:], land[:, 128:256], True, True).then_inc(s_ztp, 1)
@@ -127,11 +143,14 @@ def rank_program(g, core, T, topo):
     S.activation(T.acol[:, 0:1], T.nmo[:, 0:1], EXP, bias=nM, scale=-1.0).then_inc(s_a, 1)
     wait(V, s_wtpps)
     V.tensor_copy(T.wtp[:, 0:128], T.wtpps[:, 0:128]).then_inc(s_wtp, 1)
-    wait(PE, s_etp)
-    PE.transpose(T.epps[:, 0:64], T.etp[0:64, :], ident[0:64, 0:64]).then_inc(s_epps, 1)
+    V.wait_ge(sem.arr1b, n1)
+    wait(V, s_ior)
+    V.tensor_scalar(T.etp[64:128, :], T.iorow[64:128, :], land[64:128, 256:257], None, A.is_equal).then_inc(s_ohp, 1)
+    wait(PE, s_etp, s_ohp)
+    PE.transpose(T.epps[:, 0:128], T.etp[:], ident[:]).then_inc(s_epps, 1)
     wait(V, s_epps)
-    V.tensor_copy(land[:, 0:64], T.epps[:, 0:64]).then_inc(s_ep, 1)
-    wait(PE, s_ep, s_wtp, s_c2)
+    V.tensor_copy(land[:, 0:128], T.epps[:, 0:128]).then_inc(s_ep, 1)
+    wait(PE, s_ep, s_wtp, s_c2, s_idx)
     PE.matmul(T.up[:, 0:129], land[:, 0:128], T.wtp[:, 0:129], True, True).then_inc(s_up, 1)
     wait(V, s_a, s_uo)
     V.tensor_scalar(T.tmp[:, 0:129], T.uo[:, 0:129], T.acol[:, 0:1], None, A.mult).then_inc(s_tmp, 1)
@@ -181,4 +200,4 @@ def rank_program(g, core, T, topo):
     wait(SY, s_dsb)
     SY.dma_start(T.d[:], T.dsb[:]).then_inc(sem.stored, 16)
     SY.wait_ge(sem.stored, 16)
-    g.wait_ge(sem.sent, n1 + 2 * half)
+    g.wait_ge(sem.sent, 2 * n1 + 2 * half)

@@ -2,7 +2,7 @@ from concourse.bass import DstId, RemoteDMATransfer
 from concourse.mybir import AluOpType, AxisListType, ActivationFunctionType
 
 SLOT = 136
-NS = 56
+NS = 64
 
 SCRATCH = {
     "own":   ("sbuf", [128, 264], "bfloat16"),
@@ -17,8 +17,8 @@ SCRATCH = {
     "wto":   ("sbuf", [128, 136], "bfloat16"),
     "wtp":   ("sbuf", [128, 136], "bfloat16"),
     "eto":   ("sbuf", [128, 128], "bfloat16"),
-    "etp":   ("sbuf", [128, 128], "bfloat16"),
-    "nmo":   ("sbuf", [128, 8], "bfloat16"),
+    "oht":   ("sbuf", [128, 128], "bfloat16"),
+    "lm":    ("sbuf", [128, 128], "bfloat16"),
     "acol":  ("sbuf", [128, 4], "float32"),
     "tmp":   ("sbuf", [128, 132], "float32"),
     "X":     ("sbuf", [128, 3 * SLOT], "bfloat16"),
@@ -30,19 +30,24 @@ SCRATCH = {
     "D":     ("sbuf", [128, 192], "bfloat16"),
     "dsb":   ("sbuf", [128, 64], "bfloat16"),
     "zto":   ("psum", [128, 512], "float32"),
-    "ztp":   ("psum", [128, 512], "float32"),
+    "zp":    ("psum", [128, 512], "float32"),
     "uo":    ("psum", [128, 512], "float32"),
     "up":    ("psum", [128, 512], "float32"),
     "wtops": ("psum", [128, 1024], "bfloat16"),
     "wtpps": ("psum", [128, 1024], "bfloat16"),
     "eops":  ("psum", [128, 1024], "bfloat16"),
-    "epps":  ("psum", [128, 1024], "bfloat16"),
+    "ohps":  ("psum", [128, 1024], "bfloat16"),
 }
-SEMAPHORES = ["ld_w", "ld_oh", "ld_h", "arr1", "arr1b", "arr2", "sent", "stored"] + ["s%d" % i for i in range(NS)]
+SEMAPHORES = (["ld_w", "ld_oh", "ld_h", "arr1", "arr1b", "arr2a", "arr2", "sent", "stored"]
+              + ["s%d" % i for i in range(NS)])
 
 
 def _bits(mask):
     return [b for b in range(16) if (mask >> b) & 1]
+
+
+def _mask(bits):
+    return sum(1 << b for b in bits)
 
 
 def rank_program(g, core, T, topo):
@@ -71,115 +76,124 @@ def rank_program(g, core, T, topo):
     own, land, hb, ident, X = T.own, T.land, T.hb, T.ident, T.X
     nM = X[:, o + 129:o + 130]
     nM_t = X[0:64, o + 129:o + 130]
+    nmo = own[:, 257:258]
+    nmo_t = own[0:64, 257:258]
 
     SY.dma_start(own[:, 128:256], T.w[:]).then_inc(sem.ld_w, 16)
     S.dma_start(own[:, 64:128], T.oh[:]).then_inc(sem.ld_oh, 16)
     SY.dma_start(hb[:], T.h[:]).then_inc(sem.ld_h, 16)
 
-    s_ones, s_id, s_c1, s_c2, s_c3, s_c4, s_sel, s_z0, s_ioc, s_ior, s_zc = (new() for _ in range(11))
+    s_ones, s_id, s_c1, s_c2, s_c3, s_c4, s_sel, s_ioc, s_ior, s_zc = (new() for _ in range(10))
     g.iota(T.iocol[:, 0:1], [[0, 1]], 1, 1, allow_small_or_imprecise_dtypes=True).then_inc(s_ioc, 1)
     V.memset(T.ones[:], 1.0).then_inc(s_ones, 1)
     V.memset(T.zc[:, 0:1], 0.0).then_inc(s_zc, 1)
-    V.memset(own[:, 0:64], 0.0).then_inc(s_z0, 1)
     wait(g, s_ones)
     g.affine_select(ident[:], T.ones[:], [[-1, 128]], A.is_equal, 0.0, 0, 1).then_inc(s_id, 1)
     wait(S, s_zc)
     S.activation(T.wto[:, 128:129], T.zc[:, 0:1], EXP).then_inc(s_c1, 1)
     S.activation(T.wtp[:, 128:129], T.zc[:, 0:1], EXP).then_inc(s_c2, 1)
-    V.memset(T.nmo[64:128, 0:1], 0.0).then_inc(s_c3, 1)
+    V.memset(own[64:128, 256:258], 0.0).then_inc(s_c3, 1)
     V.memset(X[64:128, o + 129:o + 130], 0.0).then_inc(s_c4, 1)
 
-    rid, pid = topo.addr(partner, core)
-    m1 = topo.mask(core, partner)
-    n1 = len(_bits(m1))
+    rid1, pid1 = topo.addr(partner, core)
+    b1 = _bits(topo.mask(core, partner))
+    h1 = len(b1) // 2
     g.wait_ge(sem.ld_w, 16)
     g.remote_dma(out_ap=land[:, 128:256], in_ap=own[:, 128:256], remote_sem=sem.arr1, local_sem=sem.sent,
-                 pid=pid, routing_id=rid, dma_engine_mask=m1)
+                 pid=pid1, routing_id=rid1, dma_engine_mask=_mask(b1[:h1]))
     g.iota(T.iorow[:], [[1, 128]], 1, 0, allow_small_or_imprecise_dtypes=True).then_inc(s_ior, 1)
 
     s_ips, s_idx = new(), new()
+    s_zto, s_wtops, s_nmo, s_eto, s_wto, s_eops, s_eo, s_uo = (new() for _ in range(8))
     PE.wait_ge(sem.ld_oh, 16)
-    wait(PE, s_z0, s_ioc)
-    PE.matmul(T.up[:, 256:257], own[:, 0:128], T.iocol[:, 0:1], True, True).then_inc(s_ips, 1)
-    wait(V, s_ips)
-    V.tensor_copy(own[:, 256:257], T.up[:, 256:257]).then_inc(s_idx, 1)
-    wait(V, s_id)
-    V.tensor_tensor(T.sel[:], ident[:, 0:64], ident[:, 64:128], A.subtract).then_inc(s_sel, 1)
-    wait(g, s_idx)
-    g.remote_dma(out_ap=land[:, 256:257], in_ap=own[:, 256:257], remote_sem=sem.arr1b, local_sem=sem.sent,
-                 pid=pid, routing_id=rid, dma_engine_mask=m1)
-
-    s_zto, s_wtops, s_nmo, s_eto, s_wto, s_mcol, s_eops, s_eo, s_uo = (new() for _ in range(9))
+    wait(PE, s_ioc)
+    PE.matmul(T.up[0:64, 256:257], own[:, 64:128], T.iocol[:, 0:1], True, True).then_inc(s_ips, 1)
     PE.wait_ge(sem.ld_w, 16)
     PE.wait_ge(sem.ld_h, 16)
     PE.matmul(T.zto[0:64, 0:128], hb[:], own[:, 128:256], True, True).then_inc(s_zto, 1)
     wait(PE, s_id)
     PE.transpose(T.wtops[:, 0:128], own[:, 128:256], ident[:]).then_inc(s_wtops, 1)
+    wait(V, s_ips)
+    V.tensor_copy(own[0:64, 256:257], T.up[0:64, 256:257]).then_inc(s_idx, 1)
     wait(V, s_zto)
-    V.tensor_reduce(T.nmo[0:64, 0:1], T.zto[0:64, 0:128], AX, A.max, negate=True).then_inc(s_nmo, 1)
+    V.tensor_reduce(nmo_t, T.zto[0:64, 0:128], AX, A.max, negate=True).then_inc(s_nmo, 1)
+    wait(g, s_idx, s_nmo, s_c3)
+    g.remote_dma(out_ap=land[:, 256:258], in_ap=own[:, 256:258], remote_sem=sem.arr1b, local_sem=sem.sent,
+                 pid=pid1, routing_id=rid1, dma_engine_mask=_mask(b1[h1:]))
     wait(S, s_zto, s_nmo)
-    S.activation(T.eto[0:64, :], T.zto[0:64, 0:128], EXP, bias=T.nmo[0:64, 0:1], scale=1.0).then_inc(s_eto, 1)
+    S.activation(T.eto[0:64, :], T.zto[0:64, 0:128], EXP, bias=nmo_t, scale=1.0).then_inc(s_eto, 1)
     wait(V, s_wtops)
     V.tensor_copy(T.wto[:, 0:128], T.wtops[:, 0:128]).then_inc(s_wto, 1)
-    wait(V, s_nmo)
-    V.tensor_scalar(T.ztp[0:64, 128:129], T.nmo[0:64, 0:1], -1.0, None, A.mult).then_inc(s_mcol, 1)
+    wait(V, s_id)
+    V.tensor_tensor(T.sel[:], ident[:, 0:64], ident[:, 64:128], A.subtract).then_inc(s_sel, 1)
     wait(PE, s_eto)
     PE.transpose(T.eops[:, 0:64], T.eto[0:64, :], ident[0:64, 0:64]).then_inc(s_eops, 1)
-    wait(V, s_eops, s_z0)
+    wait(V, s_eops)
     V.tensor_copy(own[:, 0:64], T.eops[:, 0:64]).then_inc(s_eo, 1)
     wait(PE, s_eo, s_wto, s_c1)
     PE.matmul(T.uo[:, 0:129], own[:, 0:128], T.wto[:, 0:129], True, True).then_inc(s_uo, 1)
 
-    s_ztp, s_wtpps, s_nM, s_etp, s_ohp, s_a, s_wtp, s_epps, s_ep, s_up, s_tmp, s_msg = (new() for _ in range(12))
-    PE.wait_ge(sem.arr1, n1)
-    wait(PE, s_mcol)
-    PE.matmul(T.ztp[0:64, 0:128], hb[:], land[:, 128:256], True, True).then_inc(s_ztp, 1)
-    PE.transpose(T.wtpps[:, 0:128], land[:, 128:256], ident[:]).then_inc(s_wtpps, 1)
-    wait(V, s_ztp, s_mcol)
-    V.tensor_reduce(nM_t, T.ztp[0:64, 0:129], AX, A.max, negate=True).then_inc(s_nM, 1)
-    wait(S, s_ztp, s_nM)
-    S.activation(T.etp[0:64, :], T.ztp[0:64, 0:128], EXP, bias=nM_t, scale=1.0).then_inc(s_etp, 1)
-    wait(S, s_c3, s_c4)
-    S.activation(T.acol[:, 0:1], T.nmo[:, 0:1], EXP, bias=nM, scale=-1.0).then_inc(s_a, 1)
-    wait(V, s_wtpps)
-    V.tensor_copy(T.wtp[:, 0:128], T.wtpps[:, 0:128]).then_inc(s_wtp, 1)
-    V.wait_ge(sem.arr1b, n1)
+    s_nM, s_lm, s_oht, s_ohps, s_ohc, s_a, s_tmp = (new() for _ in range(7))
+    V.wait_ge(sem.arr1b, len(b1) - h1)
+    wait(V, s_nmo)
+    V.tensor_tensor(nM_t, nmo_t, land[0:64, 257:258], A.min).then_inc(s_nM, 1)
+    wait(V, s_nM, s_ones)
+    V.tensor_scalar(T.lm[0:64, :], T.ones[0:64, :], nM_t, None, A.mult).then_inc(s_lm, 1)
     wait(V, s_ior)
-    V.tensor_scalar(T.etp[64:128, :], T.iorow[64:128, :], land[64:128, 256:257], None, A.is_equal).then_inc(s_ohp, 1)
-    wait(PE, s_etp, s_ohp)
-    PE.transpose(T.epps[:, 0:128], T.etp[:], ident[:]).then_inc(s_epps, 1)
-    wait(V, s_epps)
-    V.tensor_copy(land[:, 0:128], T.epps[:, 0:128]).then_inc(s_ep, 1)
-    wait(PE, s_ep, s_wtp, s_c2, s_idx)
-    PE.matmul(T.up[:, 0:129], land[:, 0:128], T.wtp[:, 0:129], True, True).then_inc(s_up, 1)
+    V.tensor_scalar(T.oht[0:64, :], T.iorow[0:64, :], land[0:64, 256:257], None, A.is_equal).then_inc(s_oht, 1)
+    b2 = _bits(topo.mask(core, peers[0]) & topo.mask(core, peers[1]))
+    half = len(b2) // 2
+
+    def to_peers(ap, rsem):
+        tr = []
+        for j, p in enumerate(peers):
+            rid, pid = topo.addr(p, core)
+            tr.append(RemoteDMATransfer(dst_ids=[DstId(rid=rid, pnc=pid)], dma_engine_mask=_mask(b2[j * half:(j + 1) * half]),
+                                        remote_sem=rsem, src=ap, dst=ap))
+        g.remote_dma_fused(tr, local_sem=sem.sent)
+
+    wait(g, s_nM, s_c4)
+    to_peers(nM, sem.arr2a)
+    wait(PE, s_lm)
+    PE.matmul(T.zp[:, 0:64], T.lm[0:64, :], ident[0:64, 0:64], True, False)
+    wait(PE, s_oht)
+    PE.transpose(T.ohps[:, 0:64], T.oht[0:64, :], ident[0:64, 0:64]).then_inc(s_ohps, 1)
+    wait(V, s_ohps)
+    V.tensor_copy(land[:, 64:128], T.ohps[:, 0:64]).then_inc(s_ohc, 1)
+    wait(S, s_nM, s_c3, s_c4)
+    S.activation(T.acol[:, 0:1], nmo, EXP, bias=nM, scale=-1.0).then_inc(s_a, 1)
     wait(V, s_a, s_uo)
     V.tensor_scalar(T.tmp[:, 0:129], T.uo[:, 0:129], T.acol[:, 0:1], None, A.mult).then_inc(s_tmp, 1)
+
+    s_zp, s_wtpps, s_ep, s_wtp, s_up, s_msg = (new() for _ in range(6))
+    PE.wait_ge(sem.arr1, h1)
+    PE.matmul(T.zp[:, 0:64], land[:, 128:256], hb[:], False, True).then_inc(s_zp, 1)
+    PE.transpose(T.wtpps[:, 0:128], land[:, 128:256], ident[:]).then_inc(s_wtpps, 1)
+    wait(S, s_zp)
+    S.activation(land[:, 0:64], T.zp[:, 0:64], EXP).then_inc(s_ep, 1)
+    wait(V, s_wtpps)
+    V.tensor_copy(T.wtp[:, 0:128], T.wtpps[:, 0:128]).then_inc(s_wtp, 1)
+    wait(PE, s_ep, s_wtp, s_ohc, s_c2, s_idx)
+    PE.matmul(T.up[:, 0:129], land[:, 0:128], T.wtp[:, 0:129], True, True).then_inc(s_up, 1)
     wait(V, s_up, s_tmp)
     V.tensor_tensor(X[:, o:o + 129], T.up[:, 0:129], T.tmp[:, 0:129], A.add).then_inc(s_msg, 1)
 
-    wait(g, s_msg, s_nM, s_c4)
-    bits = _bits(topo.mask(core, peers[0]) & topo.mask(core, peers[1]))
-    half = len(bits) // 2
-    transfers = []
-    for j, p in enumerate(peers):
-        rid, pid = topo.addr(p, core)
-        transfers.append(RemoteDMATransfer(dst_ids=[DstId(rid=rid, pnc=pid)],
-                                           dma_engine_mask=sum(1 << b for b in bits[j * half:(j + 1) * half]),
-                                           remote_sem=sem.arr2, src=X[:, o:o + 130], dst=X[:, o:o + 130]))
-    g.remote_dma_fused(transfers, local_sem=sem.sent)
+    wait(g, s_msg)
+    to_peers(X[:, o:o + 129], sem.arr2)
 
     s_f1, s_ex, s_es, s_ss, s_rs, s_dsb = (new() for _ in range(6))
     s_D = [new() for _ in range(3)]
     s_mm = [new() for _ in range(3)]
     nms = X[:, 129:3 * SLOT:SLOT]
     sms = X[:, 128:3 * SLOT:SLOT]
-    V.wait_ge(sem.arr2, 2 * half)
-    wait(V, s_msg, s_nM, s_c4)
+    V.wait_ge(sem.arr2a, 2 * half)
+    wait(V, s_nM, s_c4)
     V.tensor_reduce(T.nmf[:, 0:1], nms, AX, A.min).then_inc(s_f1, 1)
-    S.wait_ge(sem.arr2, 2 * half)
+    S.wait_ge(sem.arr2a, 2 * half)
     wait(S, s_f1)
     S.activation(T.ex[:, 0:3], nms, EXP, bias=T.nmf[:, 0:1], scale=-1.0).then_inc(s_ex, 1)
-    wait(V, s_ex)
+    V.wait_ge(sem.arr2, 2 * half)
+    wait(V, s_ex, s_msg)
     V.tensor_tensor(T.es[:, 0:3], T.ex[:, 0:3], sms, A.mult).then_inc(s_es, 1)
     wait(V, s_es)
     V.tensor_reduce(T.ssum[:, 0:1], T.es[:, 0:3], AX, A.add).then_inc(s_ss, 1)
@@ -200,4 +214,4 @@ def rank_program(g, core, T, topo):
     wait(SY, s_dsb)
     SY.dma_start(T.d[:], T.dsb[:]).then_inc(sem.stored, 16)
     SY.wait_ge(sem.stored, 16)
-    g.wait_ge(sem.sent, 2 * n1 + 2 * half)
+    g.wait_ge(sem.sent, len(b1) + 4 * half)

@@ -5,8 +5,9 @@ SLOT = 136
 NS = 64
 
 SCRATCH = {
-    "own":   ("sbuf", [128, 264], "bfloat16"),
-    "land":  ("sbuf", [128, 264], "bfloat16"),
+    "own":   ("sbuf", [128, 256], "bfloat16"),
+    "land":  ("sbuf", [128, 256], "bfloat16"),
+    "nt":    ("sbuf", [128, 8], "float32"),
     "hb":    ("sbuf", [128, 64], "bfloat16"),
     "ones":  ("sbuf", [128, 128], "bfloat16"),
     "zc":    ("sbuf", [128, 8], "bfloat16"),
@@ -14,13 +15,14 @@ SCRATCH = {
     "iocol": ("sbuf", [128, 8], "bfloat16"),
     "iorow": ("sbuf", [128, 128], "bfloat16"),
     "sel":   ("sbuf", [128, 64], "bfloat16"),
-    "wto":   ("sbuf", [128, 136], "bfloat16"),
-    "wtp":   ("sbuf", [128, 136], "bfloat16"),
+    "wto":   ("sbuf", [128, 128], "bfloat16"),
+    "wtp":   ("sbuf", [128, 128], "bfloat16"),
     "eto":   ("sbuf", [128, 128], "bfloat16"),
     "oht":   ("sbuf", [128, 128], "bfloat16"),
     "lm":    ("sbuf", [128, 128], "bfloat16"),
-    "acol":  ("sbuf", [128, 4], "float32"),
-    "tmp":   ("sbuf", [128, 132], "float32"),
+    "ab":    ("sbuf", [128, 4], "float32"),
+    "t1":    ("sbuf", [128, 4], "float32"),
+    "tmp":   ("sbuf", [128, 128], "float32"),
     "X":     ("sbuf", [128, 3 * SLOT], "bfloat16"),
     "nmf":   ("sbuf", [128, 4], "float32"),
     "ex":    ("sbuf", [128, 4], "float32"),
@@ -73,27 +75,25 @@ def rank_program(g, core, T, topo):
     peers = [c for c in group if c != core]
     o = group.index(core) * SLOT
 
-    own, land, hb, ident, X = T.own, T.land, T.hb, T.ident, T.X
+    own, land, hb, ident, X, nt = T.own, T.land, T.hb, T.ident, T.X, T.nt
     nM = X[:, o + 129:o + 130]
     nM_t = X[0:64, o + 129:o + 130]
-    nmo = own[:, 257:258]
-    nmo_t = own[0:64, 257:258]
+    nmo_t = nt[0:64, 1:2]
 
     SY.dma_start(own[:, 128:256], T.w[:]).then_inc(sem.ld_w, 16)
-    S.dma_start(own[:, 64:128], T.oh[:]).then_inc(sem.ld_oh, 16)
-    SY.dma_start(hb[:], T.h[:]).then_inc(sem.ld_h, 16)
+    S.dma_start(hb[:], T.h[:]).then_inc(sem.ld_h, 16)
+    SY.dma_start(own[:, 64:128], T.oh[:]).then_inc(sem.ld_oh, 16)
 
-    s_ones, s_id, s_c1, s_c2, s_c3, s_c4, s_sel, s_ioc, s_ior, s_zc = (new() for _ in range(10))
+    s_ones, s_id, s_c1, s_c3, s_c4, s_sel, s_ioc, s_ior, s_zc = (new() for _ in range(9))
     g.iota(T.iocol[:, 0:1], [[0, 1]], 1, 1, allow_small_or_imprecise_dtypes=True).then_inc(s_ioc, 1)
     V.memset(T.ones[:], 1.0).then_inc(s_ones, 1)
     V.memset(T.zc[:, 0:1], 0.0).then_inc(s_zc, 1)
     wait(g, s_ones)
     g.affine_select(ident[:], T.ones[:], [[-1, 128]], A.is_equal, 0.0, 0, 1).then_inc(s_id, 1)
     wait(S, s_zc)
-    S.activation(T.wto[:, 128:129], T.zc[:, 0:1], EXP).then_inc(s_c1, 1)
-    S.activation(T.wtp[:, 128:129], T.zc[:, 0:1], EXP).then_inc(s_c2, 1)
-    V.memset(own[64:128, 256:258], 0.0).then_inc(s_c3, 1)
-    V.memset(X[64:128, o + 129:o + 130], 0.0).then_inc(s_c4, 1)
+    S.activation(T.rs[64:128, 0:1], T.zc[64:128, 0:1], EXP).then_inc(s_c1, 1)
+    V.memset(nt[64:128, 0:3], 0.0).then_inc(s_c3, 1)
+    V.memset(X[64:128, o + 128:o + 130], 0.0).then_inc(s_c4, 1)
 
     rid1, pid1 = topo.addr(partner, core)
     b1 = _bits(topo.mask(core, partner))
@@ -105,42 +105,51 @@ def rank_program(g, core, T, topo):
 
     s_ips, s_idx = new(), new()
     s_zto, s_wtops, s_nmo, s_eto, s_wto, s_eops, s_eo, s_uo = (new() for _ in range(8))
-    PE.wait_ge(sem.ld_oh, 16)
-    wait(PE, s_ioc)
-    PE.matmul(T.up[0:64, 256:257], own[:, 64:128], T.iocol[:, 0:1], True, True).then_inc(s_ips, 1)
     PE.wait_ge(sem.ld_w, 16)
     PE.wait_ge(sem.ld_h, 16)
     PE.matmul(T.zto[0:64, 0:128], hb[:], own[:, 128:256], True, True).then_inc(s_zto, 1)
+    PE.wait_ge(sem.ld_oh, 16)
+    wait(PE, s_ioc)
+    PE.matmul(T.up[0:64, 256:257], own[:, 64:128], T.iocol[:, 0:1], True, True).then_inc(s_ips, 1)
     wait(PE, s_id)
     PE.transpose(T.wtops[:, 0:128], own[:, 128:256], ident[:]).then_inc(s_wtops, 1)
-    wait(V, s_ips)
-    V.tensor_copy(own[0:64, 256:257], T.up[0:64, 256:257]).then_inc(s_idx, 1)
     wait(V, s_zto)
     V.tensor_reduce(nmo_t, T.zto[0:64, 0:128], AX, A.max, negate=True).then_inc(s_nmo, 1)
-    wait(g, s_idx, s_nmo, s_c3)
-    g.remote_dma(out_ap=land[:, 256:258], in_ap=own[:, 256:258], remote_sem=sem.arr1b, local_sem=sem.sent,
-                 pid=pid1, routing_id=rid1, dma_engine_mask=_mask(b1[h1:]))
     wait(S, s_zto, s_nmo)
-    S.activation(T.eto[0:64, :], T.zto[0:64, 0:128], EXP, bias=nmo_t, scale=1.0).then_inc(s_eto, 1)
+    S.activation(T.eto[0:64, :], T.zto[0:64, 0:128], EXP, bias=nmo_t, scale=1.0,
+                 accum_out=nt[0:64, 2:3]).then_inc(s_eto, 1)
+    wait(V, s_ips)
+    V.tensor_copy(nt[0:64, 0:1], T.up[0:64, 256:257]).then_inc(s_idx, 1)
+    wait(g, s_idx, s_nmo, s_eto, s_c3)
+    g.remote_dma(out_ap=nt[:, 4:7], in_ap=nt[:, 0:3], remote_sem=sem.arr1b, local_sem=sem.sent,
+                 pid=pid1, routing_id=rid1, dma_engine_mask=_mask(b1[h1:]))
     wait(V, s_wtops)
-    V.tensor_copy(T.wto[:, 0:128], T.wtops[:, 0:128]).then_inc(s_wto, 1)
+    V.tensor_copy(T.wto[:], T.wtops[:, 0:128]).then_inc(s_wto, 1)
     wait(V, s_id)
     V.tensor_tensor(T.sel[:], ident[:, 0:64], ident[:, 64:128], A.subtract).then_inc(s_sel, 1)
     wait(PE, s_eto)
     PE.transpose(T.eops[:, 0:64], T.eto[0:64, :], ident[0:64, 0:64]).then_inc(s_eops, 1)
     wait(V, s_eops)
     V.tensor_copy(own[:, 0:64], T.eops[:, 0:64]).then_inc(s_eo, 1)
-    wait(PE, s_eo, s_wto, s_c1)
-    PE.matmul(T.uo[:, 0:129], own[:, 0:128], T.wto[:, 0:129], True, True).then_inc(s_uo, 1)
+    wait(PE, s_eo, s_wto)
+    PE.matmul(T.uo[:, 0:128], own[:, 0:128], T.wto[:], True, True).then_inc(s_uo, 1)
 
-    s_nM, s_lm, s_oht, s_ohps, s_ohc, s_a, s_tmp = (new() for _ in range(7))
+    s_nM, s_lm, s_oht, s_ohps, s_ohc, s_ab, s_t1, s_sp, s_tmp = (new() for _ in range(9))
     V.wait_ge(sem.arr1b, len(b1) - h1)
     wait(V, s_nmo)
-    V.tensor_tensor(nM_t, nmo_t, land[0:64, 257:258], A.min).then_inc(s_nM, 1)
+    V.tensor_tensor(nM_t, nmo_t, nt[0:64, 5:6], A.min).then_inc(s_nM, 1)
     wait(V, s_nM, s_ones)
     V.tensor_scalar(T.lm[0:64, :], T.ones[0:64, :], nM_t, None, A.mult).then_inc(s_lm, 1)
+    S.wait_ge(sem.arr1b, len(b1) - h1)
+    wait(S, s_nM, s_c3, s_c4)
+    S.activation(T.ab[:, 0:2], nt[:, 1:6:4], EXP, bias=nM, scale=-1.0).then_inc(s_ab, 1)
     wait(V, s_ior)
-    V.tensor_scalar(T.oht[0:64, :], T.iorow[0:64, :], land[0:64, 256:257], None, A.is_equal).then_inc(s_oht, 1)
+    V.tensor_scalar(T.oht[0:64, :], T.iorow[0:64, :], nt[0:64, 4:5], None, A.is_equal).then_inc(s_oht, 1)
+    wait(V, s_ab, s_eto)
+    V.tensor_scalar(T.t1[0:64, 0:1], nt[0:64, 2:3], T.ab[0:64, 0:1], None, A.mult).then_inc(s_t1, 1)
+    wait(V, s_t1)
+    V.tensor_scalar(X[0:64, o + 128:o + 129], nt[0:64, 6:7], T.ab[0:64, 1:2], T.t1[0:64, 0:1],
+                    A.mult, A.add).then_inc(s_sp, 1)
     b2 = _bits(topo.mask(core, peers[0]) & topo.mask(core, peers[1]))
     half = len(b2) // 2
 
@@ -152,18 +161,16 @@ def rank_program(g, core, T, topo):
                                         remote_sem=rsem, src=ap, dst=ap))
         g.remote_dma_fused(tr, local_sem=sem.sent)
 
-    wait(g, s_nM, s_c4)
-    to_peers(nM, sem.arr2a)
+    wait(g, s_nM, s_sp, s_c4)
+    to_peers(X[:, o + 128:o + 130], sem.arr2a)
     wait(PE, s_lm)
     PE.matmul(T.zp[:, 0:64], T.lm[0:64, :], ident[0:64, 0:64], True, False)
     wait(PE, s_oht)
     PE.transpose(T.ohps[:, 0:64], T.oht[0:64, :], ident[0:64, 0:64]).then_inc(s_ohps, 1)
     wait(V, s_ohps)
     V.tensor_copy(land[:, 64:128], T.ohps[:, 0:64]).then_inc(s_ohc, 1)
-    wait(S, s_nM, s_c3, s_c4)
-    S.activation(T.acol[:, 0:1], nmo, EXP, bias=nM, scale=-1.0).then_inc(s_a, 1)
-    wait(V, s_a, s_uo)
-    V.tensor_scalar(T.tmp[:, 0:129], T.uo[:, 0:129], T.acol[:, 0:1], None, A.mult).then_inc(s_tmp, 1)
+    wait(V, s_uo)
+    V.tensor_scalar(T.tmp[:], T.uo[:, 0:128], T.ab[:, 0:1], None, A.mult).then_inc(s_tmp, 1)
 
     s_zp, s_wtpps, s_ep, s_wtp, s_up, s_msg = (new() for _ in range(6))
     PE.wait_ge(sem.arr1, h1)
@@ -172,37 +179,37 @@ def rank_program(g, core, T, topo):
     wait(S, s_zp)
     S.activation(land[:, 0:64], T.zp[:, 0:64], EXP).then_inc(s_ep, 1)
     wait(V, s_wtpps)
-    V.tensor_copy(T.wtp[:, 0:128], T.wtpps[:, 0:128]).then_inc(s_wtp, 1)
-    wait(PE, s_ep, s_wtp, s_ohc, s_c2, s_idx)
-    PE.matmul(T.up[:, 0:129], land[:, 0:128], T.wtp[:, 0:129], True, True).then_inc(s_up, 1)
+    V.tensor_copy(T.wtp[:], T.wtpps[:, 0:128]).then_inc(s_wtp, 1)
+    wait(PE, s_ep, s_wtp, s_ohc, s_idx)
+    PE.matmul(T.up[:, 0:128], land[:, 0:128], T.wtp[:], True, True).then_inc(s_up, 1)
     wait(V, s_up, s_tmp)
-    V.tensor_tensor(X[:, o:o + 129], T.up[:, 0:129], T.tmp[:, 0:129], A.add).then_inc(s_msg, 1)
+    V.tensor_tensor(X[:, o:o + 128], T.up[:, 0:128], T.tmp[:], A.add).then_inc(s_msg, 1)
 
     wait(g, s_msg)
-    to_peers(X[:, o:o + 129], sem.arr2)
+    to_peers(X[:, o:o + 128], sem.arr2)
 
     s_f1, s_ex, s_es, s_ss, s_rs, s_dsb = (new() for _ in range(6))
     s_D = [new() for _ in range(3)]
     s_mm = [new() for _ in range(3)]
     nms = X[:, 129:3 * SLOT:SLOT]
-    sms = X[:, 128:3 * SLOT:SLOT]
+    sms_t = X[0:64, 128:3 * SLOT:SLOT]
     V.wait_ge(sem.arr2a, 2 * half)
-    wait(V, s_nM, s_c4)
+    wait(V, s_nM, s_sp, s_c4)
     V.tensor_reduce(T.nmf[:, 0:1], nms, AX, A.min).then_inc(s_f1, 1)
     S.wait_ge(sem.arr2a, 2 * half)
     wait(S, s_f1)
     S.activation(T.ex[:, 0:3], nms, EXP, bias=T.nmf[:, 0:1], scale=-1.0).then_inc(s_ex, 1)
-    V.wait_ge(sem.arr2, 2 * half)
-    wait(V, s_ex, s_msg)
-    V.tensor_tensor(T.es[:, 0:3], T.ex[:, 0:3], sms, A.mult).then_inc(s_es, 1)
+    wait(V, s_ex)
+    V.tensor_tensor(T.es[0:64, 0:3], T.ex[0:64, 0:3], sms_t, A.mult).then_inc(s_es, 1)
     wait(V, s_es)
-    V.tensor_reduce(T.ssum[:, 0:1], T.es[:, 0:3], AX, A.add).then_inc(s_ss, 1)
+    V.tensor_reduce(T.ssum[0:64, 0:1], T.es[0:64, 0:3], AX, A.add).then_inc(s_ss, 1)
     wait(V, s_ss)
-    V.reciprocal(T.rs[:, 0:1], T.ssum[:, 0:1]).then_inc(s_rs, 1)
-    wait(V, s_rs, s_sel)
+    V.reciprocal(T.rs[0:64, 0:1], T.ssum[0:64, 0:1]).then_inc(s_rs, 1)
+    wait(V, s_rs, s_c1, s_sel)
     for k in range(3):
         V.tensor_scalar(T.D[:, 64 * k:64 * k + 64], T.sel[:], T.ex[:, k:k + 1], T.rs[:, 0:1],
                         A.mult, A.mult).then_inc(s_D[k], 1)
+
     PE.wait_ge(sem.arr2, 2 * half)
     wait(PE, s_msg, s_nmo)
     for k in range(3):

from concourse.bass import DstId, RemoteDMATransfer
from concourse.mybir import AluOpType, AxisListType, ActivationFunctionType

SLOT = 136
NS = 64

SCRATCH = {
    "own":   ("sbuf", [128, 256], "bfloat16"),
    "land":  ("sbuf", [128, 256], "bfloat16"),
    "nt":    ("sbuf", [128, 8], "float32"),
    "hb":    ("sbuf", [128, 64], "bfloat16"),
    "ones":  ("sbuf", [128, 128], "bfloat16"),
    "zc":    ("sbuf", [128, 8], "bfloat16"),
    "ident": ("sbuf", [128, 128], "bfloat16"),
    "iocol": ("sbuf", [128, 8], "bfloat16"),
    "iorow": ("sbuf", [128, 128], "bfloat16"),
    "sel":   ("sbuf", [128, 64], "bfloat16"),
    "wto":   ("sbuf", [128, 128], "bfloat16"),
    "wtp":   ("sbuf", [128, 128], "bfloat16"),
    "eto":   ("sbuf", [128, 128], "bfloat16"),
    "oht":   ("sbuf", [128, 128], "bfloat16"),
    "lm":    ("sbuf", [128, 128], "bfloat16"),
    "ab":    ("sbuf", [128, 4], "float32"),
    "t1":    ("sbuf", [128, 4], "float32"),
    "tmp":   ("sbuf", [128, 128], "float32"),
    "X":     ("sbuf", [128, 3 * SLOT], "bfloat16"),
    "nmf":   ("sbuf", [128, 4], "float32"),
    "ex":    ("sbuf", [128, 4], "float32"),
    "es":    ("sbuf", [128, 4], "float32"),
    "ssum":  ("sbuf", [128, 4], "float32"),
    "rs":    ("sbuf", [128, 4], "float32"),
    "D":     ("sbuf", [128, 192], "bfloat16"),
    "dsb":   ("sbuf", [128, 64], "bfloat16"),
    "zto":   ("psum", [128, 512], "float32"),
    "zp":    ("psum", [128, 512], "float32"),
    "uo":    ("psum", [128, 512], "float32"),
    "up":    ("psum", [128, 512], "float32"),
    "wtops": ("psum", [128, 1024], "bfloat16"),
    "wtpps": ("psum", [128, 1024], "bfloat16"),
    "eops":  ("psum", [128, 1024], "bfloat16"),
    "ohps":  ("psum", [128, 1024], "bfloat16"),
}
SEMAPHORES = (["ld_w", "ld_oh", "ld_h", "arr1", "arr1b", "arr2a", "arr2", "sent", "stored"]
              + ["s%d" % i for i in range(NS)])


def _bits(mask):
    return [b for b in range(16) if (mask >> b) & 1]


def _mask(bits):
    return sum(1 << b for b in bits)


def rank_program(g, core, T, topo):
    if T.rank_of(core) is None:
        return
    V, S, PE, SY = g.vector, g.scalar, g.tensor, g.sync
    A, EXP, AX = AluOpType, ActivationFunctionType.Exp, AxisListType.X
    sem = T.sem
    cnt = [0]

    def new():
        cnt[0] += 1
        return sem["s%d" % (cnt[0] - 1)]

    def wait(q, *sems):
        for s in sems:
            q.wait_ge(s, 1)

    my_rack = topo.rack(topo.host(core))
    group = [c for c in T.cores if topo.rack(topo.host(c)) == my_rack]
    partner = [c for c in T.cores if topo.rack(topo.host(c)) != my_rack
               and topo.chip(c) == topo.chip(core) and topo.may_write(core, c)][0]
    peers = [c for c in group if c != core]
    o = group.index(core) * SLOT

    own, land, hb, ident, X, nt = T.own, T.land, T.hb, T.ident, T.X, T.nt
    nM = X[:, o + 129:o + 130]
    nM_t = X[0:64, o + 129:o + 130]
    nmo_t = nt[0:64, 1:2]

    SY.dma_start(own[:, 128:256], T.w[:]).then_inc(sem.ld_w, 16)
    S.dma_start(hb[:], T.h[:]).then_inc(sem.ld_h, 16)
    SY.dma_start(own[:, 64:128], T.oh[:]).then_inc(sem.ld_oh, 16)

    s_ones, s_id, s_c1, s_c3, s_c4, s_sel, s_ioc, s_ior, s_zc = (new() for _ in range(9))
    g.iota(T.iocol[:, 0:1], [[0, 1]], 1, 1, allow_small_or_imprecise_dtypes=True).then_inc(s_ioc, 1)
    V.memset(T.ones[:], 1.0).then_inc(s_ones, 1)
    V.memset(T.zc[:, 0:1], 0.0).then_inc(s_zc, 1)
    wait(g, s_ones)
    g.affine_select(ident[:], T.ones[:], [[-1, 128]], A.is_equal, 0.0, 0, 1).then_inc(s_id, 1)
    wait(S, s_zc)
    S.activation(T.rs[64:128, 0:1], T.zc[64:128, 0:1], EXP).then_inc(s_c1, 1)
    V.memset(nt[64:128, 0:3], 0.0).then_inc(s_c3, 1)
    V.memset(X[64:128, o + 128:o + 130], 0.0).then_inc(s_c4, 1)

    rid1, pid1 = topo.addr(partner, core)
    b1 = _bits(topo.mask(core, partner))
    h1 = len(b1) // 2
    g.wait_ge(sem.ld_w, 16)
    g.remote_dma(out_ap=land[:, 128:256], in_ap=own[:, 128:256], remote_sem=sem.arr1, local_sem=sem.sent,
                 pid=pid1, routing_id=rid1, dma_engine_mask=_mask(b1[:h1]))
    g.iota(T.iorow[:], [[1, 128]], 1, 0, allow_small_or_imprecise_dtypes=True).then_inc(s_ior, 1)

    s_ips, s_idx = new(), new()
    s_zto, s_wtops, s_nmo, s_eto, s_wto, s_eops, s_eo, s_uo = (new() for _ in range(8))
    PE.wait_ge(sem.ld_w, 16)
    PE.wait_ge(sem.ld_h, 16)
    PE.matmul(T.zto[0:64, 0:128], hb[:], own[:, 128:256], True, True).then_inc(s_zto, 1)
    PE.wait_ge(sem.ld_oh, 16)
    wait(PE, s_ioc)
    PE.matmul(T.up[0:64, 256:257], own[:, 64:128], T.iocol[:, 0:1], True, True).then_inc(s_ips, 1)
    wait(PE, s_id)
    PE.transpose(T.wtops[:, 0:128], own[:, 128:256], ident[:]).then_inc(s_wtops, 1)
    wait(V, s_zto)
    V.tensor_reduce(nmo_t, T.zto[0:64, 0:128], AX, A.max, negate=True).then_inc(s_nmo, 1)
    wait(S, s_zto, s_nmo)
    S.activation(T.eto[0:64, :], T.zto[0:64, 0:128], EXP, bias=nmo_t, scale=1.0,
                 accum_out=nt[0:64, 2:3]).then_inc(s_eto, 1)
    wait(V, s_ips)
    V.tensor_copy(nt[0:64, 0:1], T.up[0:64, 256:257]).then_inc(s_idx, 1)
    wait(g, s_idx, s_nmo, s_eto, s_c3)
    g.remote_dma(out_ap=nt[:, 4:7], in_ap=nt[:, 0:3], remote_sem=sem.arr1b, local_sem=sem.sent,
                 pid=pid1, routing_id=rid1, dma_engine_mask=_mask(b1[h1:]))
    wait(V, s_wtops)
    V.tensor_copy(T.wto[:], T.wtops[:, 0:128]).then_inc(s_wto, 1)
    wait(V, s_id)
    V.tensor_tensor(T.sel[:], ident[:, 0:64], ident[:, 64:128], A.subtract).then_inc(s_sel, 1)
    wait(PE, s_eto)
    PE.transpose(T.eops[:, 0:64], T.eto[0:64, :], ident[0:64, 0:64]).then_inc(s_eops, 1)
    wait(V, s_eops)
    V.tensor_copy(own[:, 0:64], T.eops[:, 0:64]).then_inc(s_eo, 1)
    wait(PE, s_eo, s_wto)
    PE.matmul(T.uo[:, 0:128], own[:, 0:128], T.wto[:], True, True).then_inc(s_uo, 1)

    s_nM, s_lm, s_oht, s_ohps, s_ohc, s_ab, s_t1, s_sp, s_tmp = (new() for _ in range(9))
    V.wait_ge(sem.arr1b, len(b1) - h1)
    wait(V, s_nmo)
    V.tensor_tensor(nM_t, nmo_t, nt[0:64, 5:6], A.min).then_inc(s_nM, 1)
    wait(V, s_nM, s_ones)
    V.tensor_scalar(T.lm[0:64, :], T.ones[0:64, :], nM_t, None, A.mult).then_inc(s_lm, 1)
    S.wait_ge(sem.arr1b, len(b1) - h1)
    wait(S, s_nM, s_c3, s_c4)
    S.activation(T.ab[:, 0:2], nt[:, 1:6:4], EXP, bias=nM, scale=-1.0).then_inc(s_ab, 1)
    wait(V, s_ior)
    V.tensor_scalar(T.oht[0:64, :], T.iorow[0:64, :], nt[0:64, 4:5], None, A.is_equal).then_inc(s_oht, 1)
    wait(V, s_ab, s_eto)
    V.tensor_scalar(T.t1[0:64, 0:1], nt[0:64, 2:3], T.ab[0:64, 0:1], None, A.mult).then_inc(s_t1, 1)
    wait(V, s_t1)
    V.tensor_scalar(X[0:64, o + 128:o + 129], nt[0:64, 6:7], T.ab[0:64, 1:2], T.t1[0:64, 0:1],
                    A.mult, A.add).then_inc(s_sp, 1)
    b2 = _bits(topo.mask(core, peers[0]) & topo.mask(core, peers[1]))
    half = len(b2) // 2

    def to_peers(ap, rsem):
        tr = []
        for j, p in enumerate(peers):
            rid, pid = topo.addr(p, core)
            tr.append(RemoteDMATransfer(dst_ids=[DstId(rid=rid, pnc=pid)], dma_engine_mask=_mask(b2[j * half:(j + 1) * half]),
                                        remote_sem=rsem, src=ap, dst=ap))
        g.remote_dma_fused(tr, local_sem=sem.sent)

    wait(g, s_nM, s_sp, s_c4)
    to_peers(X[:, o + 128:o + 130], sem.arr2a)
    wait(PE, s_lm)
    PE.matmul(T.zp[:, 0:64], T.lm[0:64, :], ident[0:64, 0:64], True, False)
    wait(PE, s_oht)
    PE.transpose(T.ohps[:, 0:64], T.oht[0:64, :], ident[0:64, 0:64]).then_inc(s_ohps, 1)
    wait(V, s_ohps)
    V.tensor_copy(land[:, 64:128], T.ohps[:, 0:64]).then_inc(s_ohc, 1)
    wait(V, s_uo)
    V.tensor_scalar(T.tmp[:], T.uo[:, 0:128], T.ab[:, 0:1], None, A.mult).then_inc(s_tmp, 1)

    s_zp, s_wtpps, s_ep, s_wtp, s_up, s_msg = (new() for _ in range(6))
    PE.wait_ge(sem.arr1, h1)
    PE.matmul(T.zp[:, 0:64], land[:, 128:256], hb[:], False, True).then_inc(s_zp, 1)
    PE.transpose(T.wtpps[:, 0:128], land[:, 128:256], ident[:]).then_inc(s_wtpps, 1)
    wait(S, s_zp)
    S.activation(land[:, 0:64], T.zp[:, 0:64], EXP).then_inc(s_ep, 1)
    wait(V, s_wtpps)
    V.tensor_copy(T.wtp[:], T.wtpps[:, 0:128]).then_inc(s_wtp, 1)
    wait(PE, s_ep, s_wtp, s_ohc, s_idx)
    PE.matmul(T.up[:, 0:128], land[:, 0:128], T.wtp[:], True, True).then_inc(s_up, 1)
    wait(V, s_up, s_tmp)
    V.tensor_tensor(X[:, o:o + 128], T.up[:, 0:128], T.tmp[:], A.add).then_inc(s_msg, 1)

    wait(g, s_msg)
    to_peers(X[:, o:o + 128], sem.arr2)

    s_f1, s_ex, s_es, s_ss, s_rs, s_dsb = (new() for _ in range(6))
    s_D = [new() for _ in range(3)]
    s_mm = [new() for _ in range(3)]
    nms = X[:, 129:3 * SLOT:SLOT]
    sms_t = X[0:64, 128:3 * SLOT:SLOT]
    V.wait_ge(sem.arr2a, 2 * half)
    wait(V, s_nM, s_sp, s_c4)
    V.tensor_reduce(T.nmf[:, 0:1], nms, AX, A.min).then_inc(s_f1, 1)
    S.wait_ge(sem.arr2a, 2 * half)
    wait(S, s_f1)
    S.activation(T.ex[:, 0:3], nms, EXP, bias=T.nmf[:, 0:1], scale=-1.0).then_inc(s_ex, 1)
    wait(V, s_ex)
    V.tensor_tensor(T.es[0:64, 0:3], T.ex[0:64, 0:3], sms_t, A.mult).then_inc(s_es, 1)
    wait(V, s_es)
    V.tensor_reduce(T.ssum[0:64, 0:1], T.es[0:64, 0:3], AX, A.add).then_inc(s_ss, 1)
    wait(V, s_ss)
    V.reciprocal(T.rs[0:64, 0:1], T.ssum[0:64, 0:1]).then_inc(s_rs, 1)
    wait(V, s_rs, s_c1, s_sel)
    for k in range(3):
        V.tensor_scalar(T.D[:, 64 * k:64 * k + 64], T.sel[:], T.ex[:, k:k + 1], T.rs[:, 0:1],
                        A.mult, A.mult).then_inc(s_D[k], 1)

    PE.wait_ge(sem.arr2, 2 * half)
    wait(PE, s_msg, s_nmo)
    for k in range(3):
        wait(PE, s_D[k])
        PE.matmul(T.zto[:, 0:64], X[:, k * SLOT:k * SLOT + 128], T.D[:, 64 * k:64 * k + 64],
                  k == 0, k == 2).then_inc(s_mm[k], 1)
    wait(V, *s_mm)
    V.tensor_copy(T.dsb[:], T.zto[:, 0:64]).then_inc(s_dsb, 1)
    wait(SY, s_dsb)
    SY.dma_start(T.d[:], T.dsb[:]).then_inc(sem.stored, 16)
    SY.wait_ge(sem.stored, 16)
    g.wait_ge(sem.sent, len(b1) + 4 * half)
